import numpy as np
import ml_dtypes


def mxq(x, axis, fmt="e4m3"):
    dtype, down = {"e4m3": (ml_dtypes.float8_e4m3fn, 7), "e5m2": (ml_dtypes.float8_e5m2, 14)}[fmt]
    v = np.moveaxis(np.asarray(x, np.float32).astype(ml_dtypes.bfloat16).astype(np.float64), axis, -1)
    blocks = v.reshape(v.shape[:-1] + (-1, 32))
    amax = np.abs(blocks).max(-1, keepdims=True)
    byte = np.maximum(np.where(amax > 0, np.frexp(amax)[1] - 1 + 127, 0) - down, 1)
    scale = np.exp2(byte - 127.0)
    codes = (blocks / scale).astype(np.float32).astype(dtype).astype(np.float64)
    return np.moveaxis((codes * scale).reshape(v.shape), -1, axis)


WIDE = False


def mx_kscale(k):
    if not WIDE:
        return np.ones(k)
    levels = np.array([10, -10, 5, -5, 0])
    if k % 512:
        return np.exp2(np.random.permutation(np.resize(levels, k // 32))).repeat(32)
    a = np.empty((k // 512, 16))
    for p in range(k // 512):
        a[p, :8] = np.random.permutation(np.resize(levels, 8))
        for g in range(8):
            far = levels[np.abs(levels - a[p, g]) >= 10]
            a[p, g + 8] = far[np.random.randint(len(far))]
    return np.exp2(a.ravel()).repeat(32)


def f64(x):
    return np.asarray(x).astype(np.float64)


def striped(idx):
    return np.tile(idx.reshape(-1, 16).T, (8, 1)).astype(np.uint16)


def unstriped(offs):
    return offs[:16].T.reshape(-1).astype(np.int64)


def striped8(idx):
    return np.concatenate([x.reshape(-1, 16).T for x in idx]).astype(np.uint16)


def runs(offs, k):
    lists = np.stack([offs[16 * r : 16 * r + 16].T.reshape(-1) for r in range(8)]).astype(np.int64)
    return lists[np.arange(k) % 512 // 64]


def pack_weight(w):
    k, n = w.shape
    w = f64(np.asarray(w, np.float32).astype(ml_dtypes.bfloat16)).reshape(k // 32, 32, n)
    amax = np.abs(w).max(1)
    byte = np.clip(np.where(amax > 0, np.frexp(amax)[1] - 1 + 127 - 7, 1), 1, 254)
    scaled = (w * np.exp2(127.0 - byte)[:, None, :]).reshape(k, n).astype(np.float32)
    words = np.ascontiguousarray(scaled.reshape(k // 512, 128, 4, n).transpose(0, 1, 3, 2)).astype(ml_dtypes.float8_e4m3fn).view(np.uint8)
    return words, np.ascontiguousarray(byte.astype(np.uint8).reshape(k // 512, 16, n))


def unpack_weight(words, scales):
    g, p, n, _ = words.shape
    vals = np.ascontiguousarray(words).view(ml_dtypes.float8_e4m3fn).astype(np.float64) * np.repeat(np.exp2(scales.astype(np.float64) - 127.0), 8, axis=1)[..., None]
    return vals.transpose(0, 1, 3, 2).reshape(g * 512, n)


K, T, S, N, G, H, W = 512, 1024, 256, 512, 2048, 512, 128


def setup_inputs():
    n = np.random.standard_normal
    s = mx_kscale(K)[:, None]
    u = mx_kscale(K)
    packed_xT = pack_weight(n((K, T)) * s)
    packed_dT = pack_weight(n((K, G)) / s)
    packed_w1 = pack_weight(n((H, N)) / np.sqrt(2 * H) / u[:, None])
    packed_w2 = pack_weight(n((K, N)) / np.sqrt(2 * K) / s)
    perm = np.random.permutation(S)
    perm2 = np.random.permutation(S)
    perm3 = np.random.permutation(S)
    return {
        "x_words": packed_xT[0],
        "x_scales": packed_xT[1],
        "d_words": packed_dT[0],
        "d_scales": packed_dT[1],
        "gn": (np.random.uniform(0.5, 1.5, (H, 1)) * u[:, None]).astype(np.float32),
        "w1_words": packed_w1[0],
        "w1_scales": packed_w1[1],
        "w2_words": packed_w2[0],
        "w2_scales": packed_w2[1],
        "offs": striped(np.random.permutation(T)[:S]),
        "ka": striped8(np.random.randint(0, G, (8, H))),
        "kb": striped8(np.random.randint(0, G, (8, H))),
        "n1": striped(perm[:W]),
        "n2": striped(perm[W:]),
        "n3": striped(np.random.permutation(S)),
        "two": striped(np.random.permutation(T)[:S]),
        "n4": striped(perm2[:W]),
        "n5": striped(perm2[W:]),
        "n6": striped(perm3[:W]),
        "n7": striped(perm3[W:]),
    }


def reference(x_words, x_scales, d_words, d_scales, gn, w1_words, w1_scales, w2_words, w2_scales, offs, ka, kb, n1, n2, n3, two, n4, n5, n6, n7):
    d_ka = unpack_weight(d_words, d_scales)[np.arange(K)[:, None], runs(ka, K)]
    xq = unpack_weight(x_words, x_scales)[:, unstriped(offs)]
    d_kb = unpack_weight(d_words, d_scales)[np.arange(K)[:, None], runs(kb, K)]
    h = 0.0625 * (d_ka.T @ xq + d_kb.T @ xq)
    pa = h[:, unstriped(n1)]
    pb = h[:, unstriped(n2)]
    rb = pa - pb
    ra = pa + pb
    ua = np.zeros((H, S))
    ua[:, unstriped(n1)] = ra
    ub = ua.copy()
    ub[:, unstriped(n2)] = rb
    z = f64(gn) * (np.maximum(ub, ub[:, unstriped(n3)]))
    x_two = unpack_weight(x_words, x_scales)[:, unstriped(two)]
    h2 = unpack_weight(w1_words, w1_scales).T @ mxq(z, 0, "e4m3") + unpack_weight(w2_words, w2_scales).T @ x_two
    pa2 = h2[:, unstriped(n4)]
    pb2 = h2[:, unstriped(n5)]
    rb2 = pa2 - pb2
    ra2 = np.maximum(pa2, pb2)
    ua2 = np.zeros((N, S))
    ua2[:, unstriped(n6)] = ra2
    out = ua2.copy()
    out[:, unstriped(n7)] = rb2
    return out

@@ -1,0 +1,245 @@
+from contextlib import ExitStack
+
+import concourse.mybir as mybir
+
+K, T, S, N, G, H, W = 512, 1024, 256, 512, 2048, 512, 128
+FLOPS = 2 * K * S * (2 * H + 2 * N)
+
+F32 = mybir.dt.float32
+BF16 = mybir.dt.bfloat16
+I32 = mybir.dt.int32
+U32 = mybir.dt.uint32
+U16 = mybir.dt.uint16
+U8 = mybir.dt.uint8
+FP8X4 = mybir.dt.float8_e4m3fn_x4
+ALU = mybir.AluOpType
+COPY = mybir.ActivationFunctionType.Copy
+
+P = 128
+PACK = 4
+
+
+def tile_picked_atznthaarhcpmx_none_p_kernel(
+    tc, x_words, x_scales, d_words, d_scales, gn, w1_words, w1_scales, w2_words, w2_scales,
+    offs, ka, kb, n1, n2, n3, two, n4, n5, n6, n7, out,
+):
+    nc = tc.nc
+    with ExitStack() as ctx:
+        keep = ctx.enter_context(tc.tile_pool(name="keep", bufs=1))
+        psum = ctx.enter_context(tc.psum_pool(name="psum", bufs=1))
+
+        def tile(name, shape, dtype, tag=None):
+            return keep.tile(shape, dtype, name=name, tag=tag or name, align_bytes=64)
+
+        def load_list(name, src):
+            t = tile(name, list(src.shape), U16)
+            nc.sync.dma_start(t[:], src)
+            return t
+
+        def load_words(name, src):
+            t = tile(name, [P, src.shape[2]], U32)
+            nc.sync.dma_start(t[:].bitcast(I32), src[0].rearrange("p n t -> p (n t)").bitcast(I32))
+            return t
+
+        def load_scale_rows(name, src):
+            t = tile(name, [P, src.shape[2]], U8)
+            nc.vector.memset(t[:].bitcast(I32), 0)
+            nc.scalar.dma_start(t[0:P:8, :].bitcast(I32), src[0].bitcast(I32))
+            return t
+
+        def place_scale_rows(placed, picked, queues):
+            for a in range(4):
+                queues[a % len(queues)].dma_start(placed[a:P:32, :].bitcast(I32), picked[8 * a : P : 32, :].bitcast(I32))
+
+        d_bytes = load_scale_rows("d_bytes", d_scales)
+        x_bytes = load_scale_rows("x_bytes", x_scales)
+        ka_l = load_list("ka_l", ka)
+        kb_l = load_list("kb_l", kb)
+        offs_l = load_list("offs_l", offs)
+        d_codes = load_words("d_codes", d_words)
+        x_codes = load_words("x_codes", x_words)
+        n1_l = load_list("n1_l", n1)
+        n2_l = load_list("n2_l", n2)
+        gain = tile("gain", [P, PACK], F32)
+        nc.sync.dma_start(gain[:], gn.rearrange("(p t) o -> p (t o)", t=PACK))
+        n3_l = load_list("n3_l", n3)
+        two_l = load_list("two_l", two)
+        w2_codes = load_words("w2_codes", w2_words)
+        w1_codes = load_words("w1_codes", w1_words)
+        n4_l = load_list("n4_l", n4)
+        n5_l = load_list("n5_l", n5)
+        n6_l = load_list("n6_l", n6)
+        n7_l = load_list("n7_l", n7)
+
+        picked_b = tile("picked_b", [P, 2 * H + S], U8, tag="late")
+        placed_b = tile("placed_b", [P, 2 * H + S], U8)
+        nc.gpsimd.memset(placed_b[:].bitcast(I32), 0)
+        nc.vector.tensor_copy(picked_b[:, 0:H], d_bytes[:].indirect(ka_l[:]))
+        nc.vector.tensor_copy(picked_b[:, H : 2 * H], d_bytes[:].indirect(kb_l[:]))
+        nc.vector.tensor_copy(picked_b[:, 2 * H :], x_bytes[:].indirect(offs_l[:]))
+        place_scale_rows(placed_b, picked_b, [nc.sync, nc.scalar])
+
+        picked_d = tile("picked_d", [P, 2 * H], U32)
+        nc.vector.tensor_copy(picked_d[:, 0:H], d_codes[:].indirect(ka_l[:]))
+        nc.vector.tensor_copy(picked_d[:, H:], d_codes[:].indirect(kb_l[:]))
+        xq = tile("xq", [P, S], U32)
+        nc.vector.tensor_copy(xq[:], x_codes[:].indirect(offs_l[:]))
+
+        h = []
+
+        def first_product(t):
+            dw = tile("dw%d" % t, [P, 2, P], U32)
+            db = tile("db%d" % t, [P, 2, P], U8)
+            nc.vector.tensor_copy(dw[:].bitcast(I32), picked_d[:].bitcast(I32).rearrange("p (c m t) -> p c m t", c=2, t=PACK)[:, :, :, t])
+            nc.vector.tensor_copy(db[:], placed_b[:, 0 : 2 * H].rearrange("p (c m t) -> p c m t", c=2, t=PACK)[:, :, :, t])
+            acc = psum.tile([P, S], F32, name="acc_h%d" % t)
+            for c in range(2):
+                nc.tensor.matmul_mx(
+                    out=acc[:], lhsT=dw[:, c, :].bitcast(FP8X4), lhsT_scale=db[:, c, :],
+                    rhs=xq[:].bitcast(FP8X4), rhs_scale=placed_b[:, 2 * H :], start=(c == 0), stop=(c == 1),
+                )
+            ht = tile("h%d" % t, [P, S], F32)
+            if t == 0:
+                nc.scalar.activation(ht[:], acc[:], COPY, scale=0.0625)
+            else:
+                nc.vector.tensor_scalar(ht[:], acc[:], 0.0625, None, ALU.mult)
+            h.append(ht)
+
+        def gather(dst, window, offsets):
+            nc.scalar.activation(dst, window[:].indirect(offsets), COPY)
+
+        def scatter(window, offsets, src):
+            nc.scalar.activation(window[:].indirect(offsets), src, COPY)
+
+        pa = [tile("pa%d" % t, [P, W], F32) for t in range(PACK)]
+        pb = [tile("pb%d" % t, [P, W], F32) for t in range(PACK)]
+        ra = [tile("ra%d" % t, [P, W], F32) for t in range(PACK)]
+        rb = [tile("rb%d" % t, [P, W], F32) for t in range(PACK)]
+        ub = [tile("ub%d" % t, [P, S], F32) for t in range(PACK)]
+        un = [tile("un%d" % t, [P, S], F32) for t in range(PACK)]
+        top = [tile("top%d" % t, [P, S], F32) for t in range(PACK)]
+        z = tile("z", [P, S, PACK], BF16)
+        halves = [slice(0, W), slice(W, S)]
+
+        def haar(t):
+            nc.vector.tensor_tensor(ra[t][:], pa[t][:], pb[t][:], ALU.add)
+            nc.vector.tensor_tensor(rb[t][:], pa[t][:], pb[t][:], ALU.subtract)
+
+        def fetch_n3(t, u):
+            gather(un[t][:, halves[u]], ub[t], n3_l[:, u * (W // 16) : (u + 1) * (W // 16)])
+
+        def larger(t, cols):
+            nc.vector.tensor_tensor(top[t][:, cols], ub[t][:, cols], un[t][:, cols], ALU.max)
+
+        def gained(t, cols):
+            nc.vector.tensor_scalar(z[:, cols, t], top[t][:, cols], gain[:, t : t + 1], None, ALU.mult)
+
+        first_product(0)
+        first_product(1)
+        gather(pa[0][:], h[0], n1_l[:])
+        gather(pb[0][:], h[0], n2_l[:])
+        haar(0)
+        gather(pa[1][:], h[1], n1_l[:])
+        gather(pb[1][:], h[1], n2_l[:])
+        haar(1)
+        first_product(2)
+        first_product(3)
+
+        picked_2 = tile("picked_2", [P, S], U8)
+        placed_2 = tile("placed_2", [P, S], U8)
+        nc.gpsimd.memset(placed_2[:].bitcast(I32), 0)
+        x2 = tile("x2", [P, S], U32)
+        w_bytes = tile("w_bytes", [P, 2 * N], U8, tag="late")
+
+        scatter(ub[0], n1_l[:], ra[0][:])
+        gather(pa[2][:], h[2], n1_l[:])
+        scatter(ub[0], n2_l[:], rb[0][:])
+        gather(pb[2][:], h[2], n2_l[:])
+        haar(2)
+        nc.vector.tensor_copy(picked_2[:], x_bytes[:].indirect(two_l[:]))
+        place_scale_rows(placed_2, picked_2, [nc.sync])
+        nc.vector.tensor_copy(x2[:], x_codes[:].indirect(two_l[:]))
+        nc.gpsimd.memset(w_bytes[:].bitcast(I32), 0)
+        for c, src in enumerate((w2_scales, w1_scales)):
+            for q in range(4):
+                nc.sync.dma_start(w_bytes[32 * q : 32 * q + 4, c * N : (c + 1) * N].bitcast(I32), src[0, 4 * q : 4 * q + 4, :].bitcast(I32))
+
+        scatter(ub[1], n1_l[:], ra[1][:])
+        fetch_n3(0, 0)
+        scatter(ub[1], n2_l[:], rb[1][:])
+        fetch_n3(0, 1)
+        larger(0, slice(0, S))
+        gained(0, slice(0, S))
+        gather(pa[3][:], h[3], n1_l[:])
+        scatter(ub[2], n1_l[:], ra[2][:])
+        gather(pb[3][:], h[3], n2_l[:])
+        haar(3)
+        scatter(ub[2], n2_l[:], rb[2][:])
+        fetch_n3(1, 0)
+        fetch_n3(1, 1)
+        larger(1, slice(0, S))
+        gained(1, slice(0, S))
+        scatter(ub[3], n1_l[:], ra[3][:])
+        fetch_n3(2, 0)
+        fetch_n3(2, 1)
+        larger(2, slice(0, S))
+        gained(2, slice(0, S))
+        scatter(ub[3], n2_l[:], rb[3][:])
+        fetch_n3(3, 0)
+        fetch_n3(3, 1)
+        for u in range(2):
+            larger(3, halves[u])
+        for u in range(2):
+            gained(3, halves[u])
+        z_codes = tile("z_codes", [P, S], U32)
+        z_bytes = tile("z_bytes", [P, S], U8)
+        for u in range(2):
+            nc.vector.quantize_mx(out=z_codes[:, halves[u]].bitcast(FP8X4), scales=z_bytes[:, halves[u]], in_=z[:, halves[u], :].rearrange("p j t -> p (j t)"))
+
+        acc2 = [psum.tile([P, S], F32, name="acc_o%d" % t) for t in range(4)]
+        for t in range(4):
+            nc.tensor.matmul_mx(
+                out=acc2[t][:], lhsT=w2_codes[:, t * P : (t + 1) * P].bitcast(FP8X4), lhsT_scale=w_bytes[:, t * P : (t + 1) * P],
+                rhs=x2[:].bitcast(FP8X4), rhs_scale=placed_2[:], start=True, stop=False,
+            )
+        h2 = []
+        for t in range(4):
+            nc.tensor.matmul_mx(
+                out=acc2[t][:], lhsT=w1_codes[:, t * P : (t + 1) * P].bitcast(FP8X4), lhsT_scale=w_bytes[:, N + t * P : N + (t + 1) * P],
+                rhs=z_codes[:].bitcast(FP8X4), rhs_scale=z_bytes[:], start=False, stop=True,
+            )
+            ht = tile("h2_%d" % t, [P, S], F32)
+            if t == 0:
+                nc.scalar.activation(ht[:], acc2[t][:], COPY)
+            else:
+                nc.vector.tensor_copy(ht[:], acc2[t][:])
+            h2.append(ht)
+
+        pa2 = [tile("pa2_%d" % t, [P, W], F32) for t in range(4)]
+        pb2 = [tile("pb2_%d" % t, [P, W], F32) for t in range(4)]
+        ra2 = [tile("ra2_%d" % t, [P, W], F32) for t in range(4)]
+        rb2 = [tile("rb2_%d" % t, [P, W], F32) for t in range(4)]
+        res = [tile("res%d" % t, [P, S], F32) for t in range(4)]
+
+        def pair2(t):
+            nc.vector.tensor_tensor(ra2[t][:], pa2[t][:], pb2[t][:], ALU.max)
+            nc.vector.tensor_tensor(rb2[t][:], pa2[t][:], pb2[t][:], ALU.subtract)
+
+        def put7(t):
+            scatter(res[t], n7_l[:], rb2[t][:])
+            nc.sync.dma_start(out[t * P : (t + 1) * P, :], res[t][:])
+
+        for t in range(2):
+            gather(pa2[t][:], h2[t], n4_l[:])
+            gather(pb2[t][:], h2[t], n5_l[:])
+            pair2(t)
+        for t in range(2):
+            scatter(res[t], n6_l[:], ra2[t][:])
+            gather(pa2[t + 2][:], h2[t + 2], n4_l[:])
+            put7(t)
+            gather(pb2[t + 2][:], h2[t + 2], n5_l[:])
+            pair2(t + 2)
+        scatter(res[2], n6_l[:], ra2[2][:])
+        scatter(res[3], n6_l[:], ra2[3][:])
+        put7(2)
+        put7(3)

@@ -36,73 +36,73 @@ def tile_picked_atznthaarhcpmx_none_p_kernel(
             nc.sync.dma_start(t[:], src)
             return t
 
-        def load_words(name, src):
-            t = tile(name, [P, src.shape[2]], U32)
-            nc.sync.dma_start(t[:].bitcast(I32), src[0].rearrange("p n t -> p (n t)").bitcast(I32))
-            return t
+        def load_words(dst, src):
+            nc.sync.dma_start(dst.bitcast(I32), src[0].rearrange("p n t -> p (n t)").bitcast(I32))
 
         def load_scale_rows(name, src):
             t = tile(name, [P, src.shape[2]], U8)
-            nc.vector.memset(t[:].bitcast(I32), 0)
-            nc.scalar.dma_start(t[0:P:8, :].bitcast(I32), src[0].bitcast(I32))
+            rows = src[0].bitcast(I32)
+            nc.sync.dma_start(t[:].bitcast(I32), rows.unsqueeze(1).to_broadcast([rows.shape[0], 8, rows.shape[1]]))
             return t
 
         def place_scale_rows(placed, picked, queues):
             for a in range(4):
                 queues[a % len(queues)].dma_start(placed[a:P:32, :].bitcast(I32), picked[8 * a : P : 32, :].bitcast(I32))
 
-        d_bytes = load_scale_rows("d_bytes", d_scales)
+        offs_l = load_list("offs_l", offs)
         x_bytes = load_scale_rows("x_bytes", x_scales)
         ka_l = load_list("ka_l", ka)
+        d_bytes = load_scale_rows("d_bytes", d_scales)
         kb_l = load_list("kb_l", kb)
-        offs_l = load_list("offs_l", offs)
-        d_codes = load_words("d_codes", d_words)
-        x_codes = load_words("x_codes", x_words)
+        d_codes = tile("d_codes", [P, G], U32)
+        load_words(d_codes[:], d_words)
+        x_codes = tile("x_codes", [P, T], U32)
+        load_words(x_codes[:], x_words)
         n1_l = load_list("n1_l", n1)
         n2_l = load_list("n2_l", n2)
-        gain = tile("gain", [P, PACK], F32)
-        nc.sync.dma_start(gain[:], gn.rearrange("(p t) o -> p (t o)", t=PACK))
         n3_l = load_list("n3_l", n3)
         two_l = load_list("two_l", two)
-        w2_codes = load_words("w2_codes", w2_words)
-        w1_codes = load_words("w1_codes", w1_words)
         n4_l = load_list("n4_l", n4)
         n5_l = load_list("n5_l", n5)
         n6_l = load_list("n6_l", n6)
         n7_l = load_list("n7_l", n7)
+        gain = tile("gain", [P, PACK], F32)
+        nc.gpsimd.dma_start(gain[:], gn.rearrange("(p t) o -> p (t o)", t=PACK))
 
         picked_b = tile("picked_b", [P, 2 * H + S], U8, tag="late")
         placed_b = tile("placed_b", [P, 2 * H + S], U8)
         nc.gpsimd.memset(placed_b[:].bitcast(I32), 0)
+        nc.vector.tensor_copy(picked_b[:, 2 * H :], x_bytes[:].indirect(offs_l[:]))
         nc.vector.tensor_copy(picked_b[:, 0:H], d_bytes[:].indirect(ka_l[:]))
         nc.vector.tensor_copy(picked_b[:, H : 2 * H], d_bytes[:].indirect(kb_l[:]))
-        nc.vector.tensor_copy(picked_b[:, 2 * H :], x_bytes[:].indirect(offs_l[:]))
-        place_scale_rows(placed_b, picked_b, [nc.sync, nc.scalar])
+        place_scale_rows(placed_b, picked_b, [nc.scalar])
 
         picked_d = tile("picked_d", [P, 2 * H], U32)
-        nc.vector.tensor_copy(picked_d[:, 0:H], d_codes[:].indirect(ka_l[:]))
-        nc.vector.tensor_copy(picked_d[:, H:], d_codes[:].indirect(kb_l[:]))
+        dealt_d = tile("dealt_d", [P, 2, PACK, P], U32, tag="codes")
+
+        def pick_and_deal(c, codes_list):
+            cols = slice(c * H, (c + 1) * H)
+            nc.vector.tensor_copy(picked_d[:, cols], d_codes[:].indirect(codes_list[:]))
+            nc.vector.tensor_copy(dealt_d[:, c].bitcast(I32).rearrange("p t m -> p m t"), picked_d[:, cols].bitcast(I32).rearrange("p (m t) -> p m t", t=PACK))
+
+        pick_and_deal(0, ka_l)
         xq = tile("xq", [P, S], U32)
         nc.vector.tensor_copy(xq[:], x_codes[:].indirect(offs_l[:]))
+        pick_and_deal(1, kb_l)
 
         h = []
 
         def first_product(t):
-            dw = tile("dw%d" % t, [P, 2, P], U32)
             db = tile("db%d" % t, [P, 2, P], U8)
-            nc.vector.tensor_copy(dw[:].bitcast(I32), picked_d[:].bitcast(I32).rearrange("p (c m t) -> p c m t", c=2, t=PACK)[:, :, :, t])
             nc.vector.tensor_copy(db[:], placed_b[:, 0 : 2 * H].rearrange("p (c m t) -> p c m t", c=2, t=PACK)[:, :, :, t])
             acc = psum.tile([P, S], F32, name="acc_h%d" % t)
             for c in range(2):
                 nc.tensor.matmul_mx(
-                    out=acc[:], lhsT=dw[:, c, :].bitcast(FP8X4), lhsT_scale=db[:, c, :],
+                    out=acc[:], lhsT=dealt_d[:, c, t, :].bitcast(FP8X4), lhsT_scale=db[:, c, :],
                     rhs=xq[:].bitcast(FP8X4), rhs_scale=placed_b[:, 2 * H :], start=(c == 0), stop=(c == 1),
                 )
             ht = tile("h%d" % t, [P, S], F32)
-            if t == 0:
-                nc.scalar.activation(ht[:], acc[:], COPY, scale=0.0625)
-            else:
-                nc.vector.tensor_scalar(ht[:], acc[:], 0.0625, None, ALU.mult)
+            nc.vector.tensor_scalar(ht[:], acc[:], 0.0625, None, ALU.mult)
             h.append(ht)
 
         def gather(dst, window, offsets):
@@ -111,21 +111,17 @@ def tile_picked_atznthaarhcpmx_none_p_kernel(
         def scatter(window, offsets, src):
             nc.scalar.activation(window[:].indirect(offsets), src, COPY)
 
-        pa = [tile("pa%d" % t, [P, W], F32) for t in range(PACK)]
-        pb = [tile("pb%d" % t, [P, W], F32) for t in range(PACK)]
-        ra = [tile("ra%d" % t, [P, W], F32) for t in range(PACK)]
-        rb = [tile("rb%d" % t, [P, W], F32) for t in range(PACK)]
+        pa, pb = {}, {}
+        ra, rb = {}, {}
         ub = [tile("ub%d" % t, [P, S], F32) for t in range(PACK)]
-        un = [tile("un%d" % t, [P, S], F32) for t in range(PACK)]
+        un = {}
         top = [tile("top%d" % t, [P, S], F32) for t in range(PACK)]
         z = tile("z", [P, S, PACK], BF16)
         halves = [slice(0, W), slice(W, S)]
 
-        def haar(t):
-            nc.vector.tensor_tensor(ra[t][:], pa[t][:], pb[t][:], ALU.add)
-            nc.vector.tensor_tensor(rb[t][:], pa[t][:], pb[t][:], ALU.subtract)
-
         def fetch_n3(t, u):
+            if u == 0:
+                un[t] = tile("un%d" % t, [P, S], F32, tag="fetched%d" % ((t + 1) % 2))
             gather(un[t][:, halves[u]], ub[t], n3_l[:, u * (W // 16) : (u + 1) * (W // 16)])
 
         def larger(t, cols):
@@ -134,57 +130,64 @@ def tile_picked_atznthaarhcpmx_none_p_kernel(
         def gained(t, cols):
             nc.vector.tensor_scalar(z[:, cols, t], top[t][:, cols], gain[:, t : t + 1], None, ALU.mult)
 
+        def add_pair(t):
+            ra[t] = tile("ra%d" % t, [P, W], F32, tag="ra")
+            nc.vector.tensor_tensor(ra[t][:], pa[t], pb[t], ALU.add)
+
+        def sub_pair(t):
+            rb[t] = tile("rb%d" % t, [P, W], F32, tag="rb")
+            nc.vector.tensor_tensor(rb[t][:], pa[t], pb[t], ALU.subtract)
+
+        def fetch_pair(t):
+            pair = tile("pair%d" % t, [P, S], F32, tag="fetched%d" % (t % 2))
+            pa[t] = pair[:, 0:W]
+            pb[t] = pair[:, W:S]
+            gather(pa[t], h[t], n1_l[:])
+            gather(pb[t], h[t], n2_l[:])
+
         first_product(0)
         first_product(1)
-        gather(pa[0][:], h[0], n1_l[:])
-        gather(pb[0][:], h[0], n2_l[:])
-        haar(0)
-        gather(pa[1][:], h[1], n1_l[:])
-        gather(pb[1][:], h[1], n2_l[:])
-        haar(1)
+        fetch_pair(0)
+        add_pair(0)
+        sub_pair(0)
+        fetch_pair(1)
         first_product(2)
         first_product(3)
 
-        picked_2 = tile("picked_2", [P, S], U8)
         placed_2 = tile("placed_2", [P, S], U8)
         nc.gpsimd.memset(placed_2[:].bitcast(I32), 0)
-        x2 = tile("x2", [P, S], U32)
+        w_codes = tile("w_codes", [P, 2 * N], U32, tag="codes")
+        load_words(w_codes[:, 0:N], w2_words)
+        load_words(w_codes[:, N:], w1_words)
         w_bytes = tile("w_bytes", [P, 2 * N], U8, tag="late")
-
-        scatter(ub[0], n1_l[:], ra[0][:])
-        gather(pa[2][:], h[2], n1_l[:])
-        scatter(ub[0], n2_l[:], rb[0][:])
-        gather(pb[2][:], h[2], n2_l[:])
-        haar(2)
-        nc.vector.tensor_copy(picked_2[:], x_bytes[:].indirect(two_l[:]))
-        place_scale_rows(placed_2, picked_2, [nc.sync])
-        nc.vector.tensor_copy(x2[:], x_codes[:].indirect(two_l[:]))
         nc.gpsimd.memset(w_bytes[:].bitcast(I32), 0)
         for c, src in enumerate((w2_scales, w1_scales)):
             for q in range(4):
                 nc.sync.dma_start(w_bytes[32 * q : 32 * q + 4, c * N : (c + 1) * N].bitcast(I32), src[0, 4 * q : 4 * q + 4, :].bitcast(I32))
 
-        scatter(ub[1], n1_l[:], ra[1][:])
-        fetch_n3(0, 0)
-        scatter(ub[1], n2_l[:], rb[1][:])
-        fetch_n3(0, 1)
-        larger(0, slice(0, S))
-        gained(0, slice(0, S))
-        gather(pa[3][:], h[3], n1_l[:])
-        scatter(ub[2], n1_l[:], ra[2][:])
-        gather(pb[3][:], h[3], n2_l[:])
-        haar(3)
-        scatter(ub[2], n2_l[:], rb[2][:])
-        fetch_n3(1, 0)
-        fetch_n3(1, 1)
-        larger(1, slice(0, S))
-        gained(1, slice(0, S))
-        scatter(ub[3], n1_l[:], ra[3][:])
-        fetch_n3(2, 0)
-        fetch_n3(2, 1)
-        larger(2, slice(0, S))
-        gained(2, slice(0, S))
-        scatter(ub[3], n2_l[:], rb[3][:])
+        for t in range(PACK):
+            scatter(ub[t], n1_l[:], ra[t][:])
+            if t + 1 < PACK:
+                add_pair(t + 1)
+            if t == 0:
+                fetch_pair(2)
+            else:
+                fetch_n3(t - 1, 0)
+                fetch_n3(t - 1, 1)
+            scatter(ub[t], n2_l[:], rb[t][:])
+            if t + 1 < PACK:
+                sub_pair(t + 1)
+            if t > 0:
+                larger(t - 1, slice(0, S))
+                gained(t - 1, slice(0, S))
+            if t == 0:
+                picked_2 = tile("picked_2", [P, S], U8, tag="h2")
+                nc.vector.tensor_copy(picked_2[:], x_bytes[:].indirect(two_l[:]))
+                place_scale_rows(placed_2, picked_2, [nc.sync])
+            if t == 1:
+                fetch_pair(3)
+                x2 = tile("x2", [P, S], U32, tag="h3")
+                nc.vector.tensor_copy(x2[:], x_codes[:].indirect(two_l[:]))
         fetch_n3(3, 0)
         fetch_n3(3, 1)
         for u in range(2):
@@ -199,13 +202,13 @@ def tile_picked_atznthaarhcpmx_none_p_kernel(
         acc2 = [psum.tile([P, S], F32, name="acc_o%d" % t) for t in range(4)]
         for t in range(4):
             nc.tensor.matmul_mx(
-                out=acc2[t][:], lhsT=w2_codes[:, t * P : (t + 1) * P].bitcast(FP8X4), lhsT_scale=w_bytes[:, t * P : (t + 1) * P],
+                out=acc2[t][:], lhsT=w_codes[:, t * P : (t + 1) * P].bitcast(FP8X4), lhsT_scale=w_bytes[:, t * P : (t + 1) * P],
                 rhs=x2[:].bitcast(FP8X4), rhs_scale=placed_2[:], start=True, stop=False,
             )
         h2 = []
         for t in range(4):
             nc.tensor.matmul_mx(
-                out=acc2[t][:], lhsT=w1_codes[:, t * P : (t + 1) * P].bitcast(FP8X4), lhsT_scale=w_bytes[:, N + t * P : N + (t + 1) * P],
+                out=acc2[t][:], lhsT=w_codes[:, N + t * P : N + (t + 1) * P].bitcast(FP8X4), lhsT_scale=w_bytes[:, N + t * P : N + (t + 1) * P],
                 rhs=z_codes[:].bitcast(FP8X4), rhs_scale=z_bytes[:], start=False, stop=True,
             )
             ht = tile("h2_%d" % t, [P, S], F32)

@@ -86,7 +86,7 @@ def tile_picked_atznthaarhcpmx_none_p_kernel(
             nc.vector.tensor_copy(dealt_d[:, c].bitcast(I32).rearrange("p t m -> p m t"), picked_d[:, cols].bitcast(I32).rearrange("p (m t) -> p m t", t=PACK))
 
         pick_and_deal(0, ka_l)
-        xq = tile("xq", [P, S], U32)
+        xq = tile("xq", [P, S], U32, tag="tokens")
         nc.vector.tensor_copy(xq[:], x_codes[:].indirect(offs_l[:]))
         pick_and_deal(1, kb_l)
 
@@ -111,17 +111,24 @@ def tile_picked_atznthaarhcpmx_none_p_kernel(
         def scatter(window, offsets, src):
             nc.scalar.activation(window[:].indirect(offsets), src, COPY)
 
-        pa, pb = {}, {}
-        ra, rb = {}, {}
+        pair = [tile("pair%d" % t, [P, S], F32) for t in range(PACK)]
+        pa = [pair[t][:, 0:W] for t in range(PACK)]
+        pb = [pair[t][:, W:S] for t in range(PACK)]
+        ra = [tile("ra%d" % t, [P, W], F32) for t in range(PACK)]
+        rb = [tile("rb%d" % t, [P, W], F32) for t in range(PACK)]
         ub = [tile("ub%d" % t, [P, S], F32) for t in range(PACK)]
         un = {}
         top = [tile("top%d" % t, [P, S], F32) for t in range(PACK)]
         z = tile("z", [P, S, PACK], BF16)
         halves = [slice(0, W), slice(W, S)]
 
+        def haar(t):
+            nc.vector.tensor_tensor(ra[t][:], pa[t], pb[t], ALU.add)
+            nc.vector.tensor_tensor(rb[t][:], pa[t], pb[t], ALU.subtract)
+
         def fetch_n3(t, u):
             if u == 0:
-                un[t] = tile("un%d" % t, [P, S], F32, tag="fetched%d" % ((t + 1) % 2))
+                un[t] = tile("un%d" % t, [P, S], F32, tag="pair%d" % (t + 1))
             gather(un[t][:, halves[u]], ub[t], n3_l[:, u * (W // 16) : (u + 1) * (W // 16)])
 
         def larger(t, cols):
@@ -130,64 +137,54 @@ def tile_picked_atznthaarhcpmx_none_p_kernel(
         def gained(t, cols):
             nc.vector.tensor_scalar(z[:, cols, t], top[t][:, cols], gain[:, t : t + 1], None, ALU.mult)
 
-        def add_pair(t):
-            ra[t] = tile("ra%d" % t, [P, W], F32, tag="ra")
-            nc.vector.tensor_tensor(ra[t][:], pa[t], pb[t], ALU.add)
-
-        def sub_pair(t):
-            rb[t] = tile("rb%d" % t, [P, W], F32, tag="rb")
-            nc.vector.tensor_tensor(rb[t][:], pa[t], pb[t], ALU.subtract)
-
-        def fetch_pair(t):
-            pair = tile("pair%d" % t, [P, S], F32, tag="fetched%d" % (t % 2))
-            pa[t] = pair[:, 0:W]
-            pb[t] = pair[:, W:S]
-            gather(pa[t], h[t], n1_l[:])
-            gather(pb[t], h[t], n2_l[:])
-
         first_product(0)
         first_product(1)
-        fetch_pair(0)
-        add_pair(0)
-        sub_pair(0)
-        fetch_pair(1)
+        gather(pa[0], h[0], n1_l[:])
+        gather(pb[0], h[0], n2_l[:])
+        haar(0)
+        gather(pa[1], h[1], n1_l[:])
+        gather(pb[1], h[1], n2_l[:])
+        haar(1)
         first_product(2)
         first_product(3)
 
+        picked_2 = tile("picked_2", [P, S], U8, tag="db1")
         placed_2 = tile("placed_2", [P, S], U8)
         nc.gpsimd.memset(placed_2[:].bitcast(I32), 0)
+        x2 = tile("x2", [P, S], U32, tag="tokens")
         w_codes = tile("w_codes", [P, 2 * N], U32, tag="codes")
         load_words(w_codes[:, 0:N], w2_words)
         load_words(w_codes[:, N:], w1_words)
         w_bytes = tile("w_bytes", [P, 2 * N], U8, tag="late")
+
+        scatter(ub[0], n1_l[:], ra[0][:])
+        gather(pa[2], h[2], n1_l[:])
+        gather(pb[2], h[2], n2_l[:])
+        scatter(ub[0], n2_l[:], rb[0][:])
+        haar(2)
+        scatter(ub[1], n1_l[:], ra[1][:])
+        fetch_n3(0, 0)
+        fetch_n3(0, 1)
+        scatter(ub[1], n2_l[:], rb[1][:])
+        gather(pa[3], h[3], n1_l[:])
+        gather(pb[3], h[3], n2_l[:])
+        larger(0, slice(0, S))
+        gained(0, slice(0, S))
+        haar(3)
+        nc.vector.tensor_copy(picked_2[:], x_bytes[:].indirect(two_l[:]))
+        place_scale_rows(placed_2, picked_2, [nc.sync])
+        nc.vector.tensor_copy(x2[:], x_codes[:].indirect(two_l[:]))
         nc.gpsimd.memset(w_bytes[:].bitcast(I32), 0)
         for c, src in enumerate((w2_scales, w1_scales)):
             for q in range(4):
                 nc.sync.dma_start(w_bytes[32 * q : 32 * q + 4, c * N : (c + 1) * N].bitcast(I32), src[0, 4 * q : 4 * q + 4, :].bitcast(I32))
-
-        for t in range(PACK):
+        for t in (2, 3):
             scatter(ub[t], n1_l[:], ra[t][:])
-            if t + 1 < PACK:
-                add_pair(t + 1)
-            if t == 0:
-                fetch_pair(2)
-            else:
-                fetch_n3(t - 1, 0)
-                fetch_n3(t - 1, 1)
+            fetch_n3(t - 1, 0)
+            fetch_n3(t - 1, 1)
             scatter(ub[t], n2_l[:], rb[t][:])
-            if t + 1 < PACK:
-                sub_pair(t + 1)
-            if t > 0:
-                larger(t - 1, slice(0, S))
-                gained(t - 1, slice(0, S))
-            if t == 0:
-                picked_2 = tile("picked_2", [P, S], U8, tag="h2")
-                nc.vector.tensor_copy(picked_2[:], x_bytes[:].indirect(two_l[:]))
-                place_scale_rows(placed_2, picked_2, [nc.sync])
-            if t == 1:
-                fetch_pair(3)
-                x2 = tile("x2", [P, S], U32, tag="h3")
-                nc.vector.tensor_copy(x2[:], x_codes[:].indirect(two_l[:]))
+            larger(t - 1, slice(0, S))
+            gained(t - 1, slice(0, S))
         fetch_n3(3, 0)
         fetch_n3(3, 1)
         for u in range(2):

@@ -17,6 +17,10 @@ COPY = mybir.ActivationFunctionType.Copy
 
 P = 128
 PACK = 4
+BLOCK_PARTITIONS = 8
+QUADRANT = 32
+LIST_ROWS = 16
+OUT_TILES = N // P
 
 
 def tile_picked_atznthaarhcpmx_none_p_kernel(
@@ -32,22 +36,22 @@ def tile_picked_atznthaarhcpmx_none_p_kernel(
             return keep.tile(shape, dtype, name=name, tag=tag or name, align_bytes=64)
 
         def load_list(name, src):
-            t = tile(name, list(src.shape), U16)
-            nc.sync.dma_start(t[:], src)
-            return t
+            offsets = tile(name, list(src.shape), U16)
+            nc.sync.dma_start(offsets[:], src)
+            return offsets
 
         def load_words(dst, src):
             nc.sync.dma_start(dst.bitcast(I32), src[0].rearrange("p n t -> p (n t)").bitcast(I32))
 
         def load_scale_rows(name, src):
-            t = tile(name, [P, src.shape[2]], U8)
+            window = tile(name, [P, src.shape[2]], U8)
             rows = src[0].bitcast(I32)
-            nc.sync.dma_start(t[:].bitcast(I32), rows.unsqueeze(1).to_broadcast([rows.shape[0], 8, rows.shape[1]]))
-            return t
+            nc.sync.dma_start(window[:].bitcast(I32), rows.unsqueeze(1).to_broadcast([rows.shape[0], BLOCK_PARTITIONS, rows.shape[1]]))
+            return window
 
-        def place_scale_rows(placed, picked, queues):
-            for a in range(4):
-                queues[a % len(queues)].dma_start(placed[a:P:32, :].bitcast(I32), picked[8 * a : P : 32, :].bitcast(I32))
+        def place_scale_rows(placed, picked, queue):
+            for a in range(QUADRANT // BLOCK_PARTITIONS):
+                queue.dma_start(placed[a:P:QUADRANT, :].bitcast(I32), picked[BLOCK_PARTITIONS * a : P : QUADRANT, :].bitcast(I32))
 
         offs_l = load_list("offs_l", offs)
         x_bytes = load_scale_rows("x_bytes", x_scales)
@@ -75,7 +79,7 @@ def tile_picked_atznthaarhcpmx_none_p_kernel(
         nc.vector.tensor_copy(picked_b[:, 2 * H :], x_bytes[:].indirect(offs_l[:]))
         nc.vector.tensor_copy(picked_b[:, 0:H], d_bytes[:].indirect(ka_l[:]))
         nc.vector.tensor_copy(picked_b[:, H : 2 * H], d_bytes[:].indirect(kb_l[:]))
-        place_scale_rows(placed_b, picked_b, [nc.scalar])
+        place_scale_rows(placed_b, picked_b, nc.scalar)
 
         picked_d = tile("picked_d", [P, 2 * H], U32)
         dealt_d = tile("dealt_d", [P, 2, PACK, P], U32, tag="codes")
@@ -90,19 +94,26 @@ def tile_picked_atznthaarhcpmx_none_p_kernel(
         nc.vector.tensor_copy(xq[:], x_codes[:].indirect(offs_l[:]))
         pick_and_deal(1, kb_l)
 
+        every = slice(0, S)
+        halves = [slice(0, W), slice(W, S)]
+
+        def column_groups(t):
+            return halves if t == 0 else [every]
+
         h = []
 
         def first_product(t):
             db = tile("db%d" % t, [P, 2, P], U8)
             nc.vector.tensor_copy(db[:], placed_b[:, 0 : 2 * H].rearrange("p (c m t) -> p c m t", c=2, t=PACK)[:, :, :, t])
-            acc = psum.tile([P, S], F32, name="acc_h%d" % t)
-            for c in range(2):
-                nc.tensor.matmul_mx(
-                    out=acc[:], lhsT=dealt_d[:, c, t, :].bitcast(FP8X4), lhsT_scale=db[:, c, :],
-                    rhs=xq[:].bitcast(FP8X4), rhs_scale=placed_b[:, 2 * H :], start=(c == 0), stop=(c == 1),
-                )
             ht = tile("h%d" % t, [P, S], F32)
-            nc.vector.tensor_scalar(ht[:], acc[:], 0.0625, None, ALU.mult)
+            for u, cols in enumerate(column_groups(t)):
+                acc = psum.tile([P, cols.stop - cols.start], F32, name="acc_h%d_%d" % (t, u), tag="first%d" % u if t == 0 else "acc_h%d" % t)
+                for c in range(2):
+                    nc.tensor.matmul_mx(
+                        out=acc[:], lhsT=dealt_d[:, c, t, :].bitcast(FP8X4), lhsT_scale=db[:, c, :],
+                        rhs=xq[:, cols].bitcast(FP8X4), rhs_scale=placed_b[:, 2 * H :][:, cols], start=(c == 0), stop=(c == 1),
+                    )
+                nc.vector.tensor_scalar(ht[:, cols], acc[:], 0.0625, None, ALU.mult)
             h.append(ht)
 
         def gather(dst, window, offsets):
@@ -120,16 +131,25 @@ def tile_picked_atznthaarhcpmx_none_p_kernel(
         un = {}
         top = [tile("top%d" % t, [P, S], F32) for t in range(PACK)]
         z = tile("z", [P, S, PACK], BF16)
-        halves = [slice(0, W), slice(W, S)]
+
+        def fetch_pair(t):
+            gather(pa[t], h[t], n1_l[:])
+            gather(pb[t], h[t], n2_l[:])
 
         def haar(t):
             nc.vector.tensor_tensor(ra[t][:], pa[t], pb[t], ALU.add)
             nc.vector.tensor_tensor(rb[t][:], pa[t], pb[t], ALU.subtract)
 
-        def fetch_n3(t, u):
-            if u == 0:
-                un[t] = tile("un%d" % t, [P, S], F32, tag="pair%d" % (t + 1))
-            gather(un[t][:, halves[u]], ub[t], n3_l[:, u * (W // 16) : (u + 1) * (W // 16)])
+        def put_sum(t):
+            scatter(ub[t], n1_l[:], ra[t][:])
+
+        def put_difference(t):
+            scatter(ub[t], n2_l[:], rb[t][:])
+
+        def fetch_n3(t):
+            un[t] = tile("un%d" % t, [P, S], F32, tag="pair%d" % (t + 1))
+            for u in range(2):
+                gather(un[t][:, halves[u]], ub[t], n3_l[:, u * (W // LIST_ROWS) : (u + 1) * (W // LIST_ROWS)])
 
         def larger(t, cols):
             nc.vector.tensor_tensor(top[t][:, cols], ub[t][:, cols], un[t][:, cols], ALU.max)
@@ -137,16 +157,13 @@ def tile_picked_atznthaarhcpmx_none_p_kernel(
         def gained(t, cols):
             nc.vector.tensor_scalar(z[:, cols, t], top[t][:, cols], gain[:, t : t + 1], None, ALU.mult)
 
-        first_product(0)
-        first_product(1)
-        gather(pa[0], h[0], n1_l[:])
-        gather(pb[0], h[0], n2_l[:])
-        haar(0)
-        gather(pa[1], h[1], n1_l[:])
-        gather(pb[1], h[1], n2_l[:])
-        haar(1)
-        first_product(2)
-        first_product(3)
+        for t in range(2):
+            first_product(t)
+        for t in range(2):
+            fetch_pair(t)
+            haar(t)
+        for t in range(2, PACK):
+            first_product(t)
 
         picked_2 = tile("picked_2", [P, S], U8, tag="db1")
         placed_2 = tile("placed_2", [P, S], U8)
@@ -157,89 +174,89 @@ def tile_picked_atznthaarhcpmx_none_p_kernel(
         load_words(w_codes[:, N:], w1_words)
         w_bytes = tile("w_bytes", [P, 2 * N], U8, tag="late")
 
-        scatter(ub[0], n1_l[:], ra[0][:])
-        gather(pa[2], h[2], n1_l[:])
-        gather(pb[2], h[2], n2_l[:])
-        scatter(ub[0], n2_l[:], rb[0][:])
+        put_sum(0)
+        fetch_pair(2)
+        put_difference(0)
         haar(2)
-        scatter(ub[1], n1_l[:], ra[1][:])
-        fetch_n3(0, 0)
-        fetch_n3(0, 1)
-        scatter(ub[1], n2_l[:], rb[1][:])
-        gather(pa[3], h[3], n1_l[:])
-        gather(pb[3], h[3], n2_l[:])
-        larger(0, slice(0, S))
-        gained(0, slice(0, S))
+        put_sum(1)
+        fetch_n3(0)
+        put_difference(1)
+        fetch_pair(3)
+        larger(0, every)
+        gained(0, every)
         haar(3)
         nc.vector.tensor_copy(picked_2[:], x_bytes[:].indirect(two_l[:]))
-        place_scale_rows(placed_2, picked_2, [nc.sync])
+        place_scale_rows(placed_2, picked_2, nc.sync)
         nc.vector.tensor_copy(x2[:], x_codes[:].indirect(two_l[:]))
         nc.gpsimd.memset(w_bytes[:].bitcast(I32), 0)
         for c, src in enumerate((w2_scales, w1_scales)):
-            for q in range(4):
-                nc.sync.dma_start(w_bytes[32 * q : 32 * q + 4, c * N : (c + 1) * N].bitcast(I32), src[0, 4 * q : 4 * q + 4, :].bitcast(I32))
-        for t in (2, 3):
-            scatter(ub[t], n1_l[:], ra[t][:])
-            fetch_n3(t - 1, 0)
-            fetch_n3(t - 1, 1)
-            scatter(ub[t], n2_l[:], rb[t][:])
-            larger(t - 1, slice(0, S))
-            gained(t - 1, slice(0, S))
-        fetch_n3(3, 0)
-        fetch_n3(3, 1)
-        for u in range(2):
-            larger(3, halves[u])
-        for u in range(2):
-            gained(3, halves[u])
+            for q in range(P // QUADRANT):
+                nc.sync.dma_start(w_bytes[QUADRANT * q : QUADRANT * q + 4, c * N : (c + 1) * N].bitcast(I32), src[0, 4 * q : 4 * q + 4, :].bitcast(I32))
+        for t in range(2, PACK):
+            put_sum(t)
+            fetch_n3(t - 1)
+            put_difference(t)
+            larger(t - 1, every)
+            gained(t - 1, every)
+
+        last = PACK - 1
+        fetch_n3(last)
+        for cols in halves:
+            larger(last, cols)
+        for cols in halves:
+            gained(last, cols)
         z_codes = tile("z_codes", [P, S], U32)
         z_bytes = tile("z_bytes", [P, S], U8)
-        for u in range(2):
-            nc.vector.quantize_mx(out=z_codes[:, halves[u]].bitcast(FP8X4), scales=z_bytes[:, halves[u]], in_=z[:, halves[u], :].rearrange("p j t -> p (j t)"))
+        for cols in halves:
+            nc.vector.quantize_mx(out=z_codes[:, cols].bitcast(FP8X4), scales=z_bytes[:, cols], in_=z[:, cols, :].rearrange("p j t -> p (j t)"))
 
-        acc2 = [psum.tile([P, S], F32, name="acc_o%d" % t) for t in range(4)]
-        for t in range(4):
+        groups = [(t, u, cols) for t in range(OUT_TILES) for u, cols in enumerate(column_groups(t))]
+        acc2 = [
+            psum.tile([P, cols.stop - cols.start], F32, name="acc_o%d_%d" % (t, u), tag="first%d" % u if t == 0 else "acc_o%d" % t)
+            for t, u, cols in groups
+        ]
+        for acc, (t, u, cols) in zip(acc2, groups):
             nc.tensor.matmul_mx(
-                out=acc2[t][:], lhsT=w_codes[:, t * P : (t + 1) * P].bitcast(FP8X4), lhsT_scale=w_bytes[:, t * P : (t + 1) * P],
-                rhs=x2[:].bitcast(FP8X4), rhs_scale=placed_2[:], start=True, stop=False,
+                out=acc[:], lhsT=w_codes[:, t * P : (t + 1) * P].bitcast(FP8X4), lhsT_scale=w_bytes[:, t * P : (t + 1) * P],
+                rhs=x2[:, cols].bitcast(FP8X4), rhs_scale=placed_2[:, cols], start=True, stop=False,
             )
-        h2 = []
-        for t in range(4):
+        h2 = [tile("h2_%d" % t, [P, S], F32) for t in range(OUT_TILES)]
+        for acc, (t, u, cols) in zip(acc2, groups):
             nc.tensor.matmul_mx(
-                out=acc2[t][:], lhsT=w_codes[:, N + t * P : N + (t + 1) * P].bitcast(FP8X4), lhsT_scale=w_bytes[:, N + t * P : N + (t + 1) * P],
-                rhs=z_codes[:].bitcast(FP8X4), rhs_scale=z_bytes[:], start=False, stop=True,
+                out=acc[:], lhsT=w_codes[:, N + t * P : N + (t + 1) * P].bitcast(FP8X4), lhsT_scale=w_bytes[:, N + t * P : N + (t + 1) * P],
+                rhs=z_codes[:, cols].bitcast(FP8X4), rhs_scale=z_bytes[:, cols], start=False, stop=True,
             )
-            ht = tile("h2_%d" % t, [P, S], F32)
-            if t == 0:
-                nc.scalar.activation(ht[:], acc2[t][:], COPY)
-            else:
-                nc.vector.tensor_copy(ht[:], acc2[t][:])
-            h2.append(ht)
+            nc.vector.tensor_copy(h2[t][:, cols], acc[:])
 
-        pa2 = [tile("pa2_%d" % t, [P, W], F32) for t in range(4)]
-        pb2 = [tile("pb2_%d" % t, [P, W], F32) for t in range(4)]
-        ra2 = [tile("ra2_%d" % t, [P, W], F32) for t in range(4)]
-        rb2 = [tile("rb2_%d" % t, [P, W], F32) for t in range(4)]
-        res = [tile("res%d" % t, [P, S], F32) for t in range(4)]
+        pa2 = [tile("pa2_%d" % t, [P, W], F32) for t in range(OUT_TILES)]
+        pb2 = [tile("pb2_%d" % t, [P, W], F32) for t in range(OUT_TILES)]
+        ra2 = [tile("ra2_%d" % t, [P, W], F32) for t in range(OUT_TILES)]
+        rb2 = [tile("rb2_%d" % t, [P, W], F32) for t in range(OUT_TILES)]
+        res = [tile("res%d" % t, [P, S], F32) for t in range(OUT_TILES)]
 
         def pair2(t):
             nc.vector.tensor_tensor(ra2[t][:], pa2[t][:], pb2[t][:], ALU.max)
             nc.vector.tensor_tensor(rb2[t][:], pa2[t][:], pb2[t][:], ALU.subtract)
 
-        def put7(t):
+        def put_larger(t):
+            scatter(res[t], n6_l[:], ra2[t][:])
+
+        def put_difference_and_store(t):
             scatter(res[t], n7_l[:], rb2[t][:])
             nc.sync.dma_start(out[t * P : (t + 1) * P, :], res[t][:])
 
-        for t in range(2):
+        ahead = 2
+        for t in range(ahead):
             gather(pa2[t][:], h2[t], n4_l[:])
             gather(pb2[t][:], h2[t], n5_l[:])
             pair2(t)
-        for t in range(2):
-            scatter(res[t], n6_l[:], ra2[t][:])
-            gather(pa2[t + 2][:], h2[t + 2], n4_l[:])
-            put7(t)
-            gather(pb2[t + 2][:], h2[t + 2], n5_l[:])
-            pair2(t + 2)
-        scatter(res[2], n6_l[:], ra2[2][:])
-        scatter(res[3], n6_l[:], ra2[3][:])
-        put7(2)
-        put7(3)
+        for t in range(OUT_TILES - ahead):
+            put_larger(t)
+            gather(pa2[t + ahead][:], h2[t + ahead], n4_l[:])
+            put_difference_and_store(t)
+            gather(pb2[t + ahead][:], h2[t + ahead], n5_l[:])
+            pair2(t + ahead)
+        for t in range(OUT_TILES - ahead, OUT_TILES):
+            put_larger(t)
+        for t in range(OUT_TILES - ahead, OUT_TILES):
+            put_difference_and_store(t)

from contextlib import ExitStack

import concourse.mybir as mybir

K, T, S, N, G, H, W = 512, 1024, 256, 512, 2048, 512, 128
FLOPS = 2 * K * S * (2 * H + 2 * N)

F32 = mybir.dt.float32
BF16 = mybir.dt.bfloat16
I32 = mybir.dt.int32
U32 = mybir.dt.uint32
U16 = mybir.dt.uint16
U8 = mybir.dt.uint8
FP8X4 = mybir.dt.float8_e4m3fn_x4
ALU = mybir.AluOpType
COPY = mybir.ActivationFunctionType.Copy

P = 128
PACK = 4
BLOCK_PARTITIONS = 8
QUADRANT = 32
LIST_ROWS = 16
OUT_TILES = N // P


def tile_picked_atznthaarhcpmx_none_p_kernel(
    tc, x_words, x_scales, d_words, d_scales, gn, w1_words, w1_scales, w2_words, w2_scales,
    offs, ka, kb, n1, n2, n3, two, n4, n5, n6, n7, out,
):
    nc = tc.nc
    with ExitStack() as ctx:
        keep = ctx.enter_context(tc.tile_pool(name="keep", bufs=1))
        psum = ctx.enter_context(tc.psum_pool(name="psum", bufs=1))

        def tile(name, shape, dtype, tag=None):
            return keep.tile(shape, dtype, name=name, tag=tag or name, align_bytes=64)

        def load_list(name, src):
            offsets = tile(name, list(src.shape), U16)
            nc.sync.dma_start(offsets[:], src)
            return offsets

        def load_words(dst, src):
            nc.sync.dma_start(dst.bitcast(I32), src[0].rearrange("p n t -> p (n t)").bitcast(I32))

        def load_scale_rows(name, src):
            window = tile(name, [P, src.shape[2]], U8)
            rows = src[0].bitcast(I32)
            nc.sync.dma_start(window[:].bitcast(I32), rows.unsqueeze(1).to_broadcast([rows.shape[0], BLOCK_PARTITIONS, rows.shape[1]]))
            return window

        def place_scale_rows(placed, picked, queue):
            for a in range(QUADRANT // BLOCK_PARTITIONS):
                queue.dma_start(placed[a:P:QUADRANT, :].bitcast(I32), picked[BLOCK_PARTITIONS * a : P : QUADRANT, :].bitcast(I32))

        offs_l = load_list("offs_l", offs)
        x_bytes = load_scale_rows("x_bytes", x_scales)
        ka_l = load_list("ka_l", ka)
        d_bytes = load_scale_rows("d_bytes", d_scales)
        kb_l = load_list("kb_l", kb)
        d_codes = tile("d_codes", [P, G], U32)
        load_words(d_codes[:], d_words)
        x_codes = tile("x_codes", [P, T], U32)
        load_words(x_codes[:], x_words)
        n1_l = load_list("n1_l", n1)
        n2_l = load_list("n2_l", n2)
        n3_l = load_list("n3_l", n3)
        two_l = load_list("two_l", two)
        n4_l = load_list("n4_l", n4)
        n5_l = load_list("n5_l", n5)
        n6_l = load_list("n6_l", n6)
        n7_l = load_list("n7_l", n7)
        gain = tile("gain", [P, PACK], F32)
        nc.gpsimd.dma_start(gain[:], gn.rearrange("(p t) o -> p (t o)", t=PACK))

        picked_b = tile("picked_b", [P, 2 * H + S], U8, tag="late")
        placed_b = tile("placed_b", [P, 2 * H + S], U8)
        nc.gpsimd.memset(placed_b[:].bitcast(I32), 0)
        nc.vector.tensor_copy(picked_b[:, 2 * H :], x_bytes[:].indirect(offs_l[:]))
        nc.vector.tensor_copy(picked_b[:, 0:H], d_bytes[:].indirect(ka_l[:]))
        nc.vector.tensor_copy(picked_b[:, H : 2 * H], d_bytes[:].indirect(kb_l[:]))
        place_scale_rows(placed_b, picked_b, nc.scalar)

        picked_d = tile("picked_d", [P, 2 * H], U32)
        dealt_d = tile("dealt_d", [P, 2, PACK, P], U32, tag="codes")

        def pick_and_deal(c, codes_list):
            cols = slice(c * H, (c + 1) * H)
            nc.vector.tensor_copy(picked_d[:, cols], d_codes[:].indirect(codes_list[:]))
            nc.vector.tensor_copy(dealt_d[:, c].bitcast(I32).rearrange("p t m -> p m t"), picked_d[:, cols].bitcast(I32).rearrange("p (m t) -> p m t", t=PACK))

        pick_and_deal(0, ka_l)
        xq = tile("xq", [P, S], U32, tag="tokens")
        nc.vector.tensor_copy(xq[:], x_codes[:].indirect(offs_l[:]))
        pick_and_deal(1, kb_l)

        every = slice(0, S)
        halves = [slice(0, W), slice(W, S)]

        def column_groups(t):
            return halves if t == 0 else [every]

        h = []

        def first_product(t):
            db = tile("db%d" % t, [P, 2, P], U8)
            nc.vector.tensor_copy(db[:], placed_b[:, 0 : 2 * H].rearrange("p (c m t) -> p c m t", c=2, t=PACK)[:, :, :, t])
            ht = tile("h%d" % t, [P, S], F32)
            for u, cols in enumerate(column_groups(t)):
                acc = psum.tile([P, cols.stop - cols.start], F32, name="acc_h%d_%d" % (t, u), tag="first%d" % u if t == 0 else "acc_h%d" % t)
                for c in range(2):
                    nc.tensor.matmul_mx(
                        out=acc[:], lhsT=dealt_d[:, c, t, :].bitcast(FP8X4), lhsT_scale=db[:, c, :],
                        rhs=xq[:, cols].bitcast(FP8X4), rhs_scale=placed_b[:, 2 * H :][:, cols], start=(c == 0), stop=(c == 1),
                    )
                nc.vector.tensor_scalar(ht[:, cols], acc[:], 0.0625, None, ALU.mult)
            h.append(ht)

        def gather(dst, window, offsets):
            nc.scalar.activation(dst, window[:].indirect(offsets), COPY)

        def scatter(window, offsets, src):
            nc.scalar.activation(window[:].indirect(offsets), src, COPY)

        pair = [tile("pair%d" % t, [P, S], F32) for t in range(PACK)]
        pa = [pair[t][:, 0:W] for t in range(PACK)]
        pb = [pair[t][:, W:S] for t in range(PACK)]
        ra = [tile("ra%d" % t, [P, W], F32) for t in range(PACK)]
        rb = [tile("rb%d" % t, [P, W], F32) for t in range(PACK)]
        ub = [tile("ub%d" % t, [P, S], F32) for t in range(PACK)]
        un = {}
        top = [tile("top%d" % t, [P, S], F32) for t in range(PACK)]
        z = tile("z", [P, S, PACK], BF16)

        def fetch_pair(t):
            gather(pa[t], h[t], n1_l[:])
            gather(pb[t], h[t], n2_l[:])

        def haar(t):
            nc.vector.tensor_tensor(ra[t][:], pa[t], pb[t], ALU.add)
            nc.vector.tensor_tensor(rb[t][:], pa[t], pb[t], ALU.subtract)

        def put_sum(t):
            scatter(ub[t], n1_l[:], ra[t][:])

        def put_difference(t):
            scatter(ub[t], n2_l[:], rb[t][:])

        def fetch_n3(t):
            un[t] = tile("un%d" % t, [P, S], F32, tag="pair%d" % (t + 1))
            for u in range(2):
                gather(un[t][:, halves[u]], ub[t], n3_l[:, u * (W // LIST_ROWS) : (u + 1) * (W // LIST_ROWS)])

        def larger(t, cols):
            nc.vector.tensor_tensor(top[t][:, cols], ub[t][:, cols], un[t][:, cols], ALU.max)

        def gained(t, cols):
            nc.vector.tensor_scalar(z[:, cols, t], top[t][:, cols], gain[:, t : t + 1], None, ALU.mult)

        for t in range(2):
            first_product(t)
        for t in range(2):
            fetch_pair(t)
            haar(t)
        for t in range(2, PACK):
            first_product(t)

        picked_2 = tile("picked_2", [P, S], U8, tag="db1")
        placed_2 = tile("placed_2", [P, S], U8)
        nc.gpsimd.memset(placed_2[:].bitcast(I32), 0)
        x2 = tile("x2", [P, S], U32, tag="tokens")
        w_codes = tile("w_codes", [P, 2 * N], U32, tag="codes")
        load_words(w_codes[:, 0:N], w2_words)
        load_words(w_codes[:, N:], w1_words)
        w_bytes = tile("w_bytes", [P, 2 * N], U8, tag="late")

        put_sum(0)
        fetch_pair(2)
        put_difference(0)
        haar(2)
        put_sum(1)
        fetch_n3(0)
        put_difference(1)
        fetch_pair(3)
        larger(0, every)
        gained(0, every)
        haar(3)
        nc.vector.tensor_copy(picked_2[:], x_bytes[:].indirect(two_l[:]))
        place_scale_rows(placed_2, picked_2, nc.sync)
        nc.vector.tensor_copy(x2[:], x_codes[:].indirect(two_l[:]))
        nc.gpsimd.memset(w_bytes[:].bitcast(I32), 0)
        for c, src in enumerate((w2_scales, w1_scales)):
            for q in range(P // QUADRANT):
                nc.sync.dma_start(w_bytes[QUADRANT * q : QUADRANT * q + 4, c * N : (c + 1) * N].bitcast(I32), src[0, 4 * q : 4 * q + 4, :].bitcast(I32))
        for t in range(2, PACK):
            put_sum(t)
            fetch_n3(t - 1)
            put_difference(t)
            larger(t - 1, every)
            gained(t - 1, every)

        last = PACK - 1
        fetch_n3(last)
        for cols in halves:
            larger(last, cols)
        for cols in halves:
            gained(last, cols)
        z_codes = tile("z_codes", [P, S], U32)
        z_bytes = tile("z_bytes", [P, S], U8)
        for cols in halves:
            nc.vector.quantize_mx(out=z_codes[:, cols].bitcast(FP8X4), scales=z_bytes[:, cols], in_=z[:, cols, :].rearrange("p j t -> p (j t)"))

        groups = [(t, u, cols) for t in range(OUT_TILES) for u, cols in enumerate(column_groups(t))]
        acc2 = [
            psum.tile([P, cols.stop - cols.start], F32, name="acc_o%d_%d" % (t, u), tag="first%d" % u if t == 0 else "acc_o%d" % t)
            for t, u, cols in groups
        ]
        for acc, (t, u, cols) in zip(acc2, groups):
            nc.tensor.matmul_mx(
                out=acc[:], lhsT=w_codes[:, t * P : (t + 1) * P].bitcast(FP8X4), lhsT_scale=w_bytes[:, t * P : (t + 1) * P],
                rhs=x2[:, cols].bitcast(FP8X4), rhs_scale=placed_2[:, cols], start=True, stop=False,
            )
        h2 = [tile("h2_%d" % t, [P, S], F32) for t in range(OUT_TILES)]
        for acc, (t, u, cols) in zip(acc2, groups):
            nc.tensor.matmul_mx(
                out=acc[:], lhsT=w_codes[:, N + t * P : N + (t + 1) * P].bitcast(FP8X4), lhsT_scale=w_bytes[:, N + t * P : N + (t + 1) * P],
                rhs=z_codes[:, cols].bitcast(FP8X4), rhs_scale=z_bytes[:, cols], start=False, stop=True,
            )
            nc.vector.tensor_copy(h2[t][:, cols], acc[:])

        pa2 = [tile("pa2_%d" % t, [P, W], F32) for t in range(OUT_TILES)]
        pb2 = [tile("pb2_%d" % t, [P, W], F32) for t in range(OUT_TILES)]
        ra2 = [tile("ra2_%d" % t, [P, W], F32) for t in range(OUT_TILES)]
        rb2 = [tile("rb2_%d" % t, [P, W], F32) for t in range(OUT_TILES)]
        res = [tile("res%d" % t, [P, S], F32) for t in range(OUT_TILES)]

        def pair2(t):
            nc.vector.tensor_tensor(ra2[t][:], pa2[t][:], pb2[t][:], ALU.max)
            nc.vector.tensor_tensor(rb2[t][:], pa2[t][:], pb2[t][:], ALU.subtract)

        def put_larger(t):
            scatter(res[t], n6_l[:], ra2[t][:])

        def put_difference_and_store(t):
            scatter(res[t], n7_l[:], rb2[t][:])
            nc.sync.dma_start(out[t * P : (t + 1) * P, :], res[t][:])

        ahead = 2
        for t in range(ahead):
            gather(pa2[t][:], h2[t], n4_l[:])
            gather(pb2[t][:], h2[t], n5_l[:])
            pair2(t)
        for t in range(OUT_TILES - ahead):
            put_larger(t)
            gather(pa2[t + ahead][:], h2[t + ahead], n4_l[:])
            put_difference_and_store(t)
            gather(pb2[t + ahead][:], h2[t + ahead], n5_l[:])
            pair2(t + ahead)
        for t in range(OUT_TILES - ahead, OUT_TILES):
            put_larger(t)
        for t in range(OUT_TILES - ahead, OUT_TILES):
            put_difference_and_store(t)
